import numpy as np
import ml_dtypes


def mxq(x, axis, fmt="e4m3"):
    dtype, down = {"e4m3": (ml_dtypes.float8_e4m3fn, 7), "e5m2": (ml_dtypes.float8_e5m2, 14)}[fmt]
    v = np.moveaxis(np.asarray(x, np.float32).astype(ml_dtypes.bfloat16).astype(np.float64), axis, -1)
    blocks = v.reshape(v.shape[:-1] + (-1, 32))
    amax = np.abs(blocks).max(-1, keepdims=True)
    byte = np.maximum(np.where(amax > 0, np.frexp(amax)[1] - 1 + 127, 0) - down, 1)
    scale = np.exp2(byte - 127.0)
    codes = (blocks / scale).astype(np.float32).astype(dtype).astype(np.float64)
    return np.moveaxis((codes * scale).reshape(v.shape), -1, axis)


WIDE = False


def mx_kscale(k):
    if not WIDE:
        return np.ones(k)
    levels = np.array([10, -10, 5, -5, 0])
    if k % 512:
        return np.exp2(np.random.permutation(np.resize(levels, k // 32))).repeat(32)
    a = np.empty((k // 512, 16))
    for p in range(k // 512):
        a[p, :8] = np.random.permutation(np.resize(levels, 8))
        for g in range(8):
            far = levels[np.abs(levels - a[p, g]) >= 10]
            a[p, g + 8] = far[np.random.randint(len(far))]
    return np.exp2(a.ravel()).repeat(32)


def f64(x):
    return np.asarray(x).astype(np.float64)


def striped(idx):
    return np.tile(idx.reshape(-1, 16).T, (8, 1)).astype(np.uint16)


def unstriped(offs):
    return offs[:16].T.reshape(-1).astype(np.int64)


def striped8(idx):
    return np.concatenate([x.reshape(-1, 16).T for x in idx]).astype(np.uint16)


def runs(offs, k):
    lists = np.stack([offs[16 * r : 16 * r + 16].T.reshape(-1) for r in range(8)]).astype(np.int64)
    return lists[np.arange(k) % 512 // 64]


def pack_weight(w):
    k, n = w.shape
    w = f64(np.asarray(w, np.float32).astype(ml_dtypes.bfloat16)).reshape(k // 32, 32, n)
    amax = np.abs(w).max(1)
    byte = np.clip(np.where(amax > 0, np.frexp(amax)[1] - 1 + 127 - 7, 1), 1, 254)
    scaled = (w * np.exp2(127.0 - byte)[:, None, :]).reshape(k, n).astype(np.float32)
    words = np.ascontiguousarray(scaled.reshape(k // 512, 128, 4, n).transpose(0, 1, 3, 2)).astype(ml_dtypes.float8_e4m3fn).view(np.uint8)
    return words, np.ascontiguousarray(byte.astype(np.uint8).reshape(k // 512, 16, n))


def unpack_weight(words, scales):
    g, p, n, _ = words.shape
    vals = np.ascontiguousarray(words).view(ml_dtypes.float8_e4m3fn).astype(np.float64) * np.repeat(np.exp2(scales.astype(np.float64) - 127.0), 8, axis=1)[..., None]
    return vals.transpose(0, 1, 3, 2).reshape(g * 512, n)


def relu(v):
    return np.maximum(v, 0.0)


K, T, S, N, H, U = 512, 2048, 512, 512, 512, 512


def setup_inputs():
    n = np.random.standard_normal
    s = mx_kscale(K)[:, None]
    u = mx_kscale(H)
    packed_xT = pack_weight(n((K, T)) * s)
    return {
        "x_words": packed_xT[0],
        "x_scales": packed_xT[1],
        "w1": (n((K, H)) / np.sqrt(K) / s).astype(np.float32),
        "cf1": (n((H, U)) * u[:, None]).astype(np.float32),
        "cf2": (n((H, U)) * u[:, None]).astype(np.float32),
        "cf3": (n((H, U)) * u[:, None]).astype(np.float32),
        "w2": (n((H, N)) / np.sqrt(H) / u[:, None]).astype(np.float32),
        "offs": striped(np.random.permutation(T)[:S]),
        "fn": striped8(np.random.randint(0, U, (8, S))),
    }


def reference(x_words, x_scales, w1, cf1, cf2, cf3, w2, offs, fn):
    xq = unpack_weight(x_words, x_scales)[:, unstriped(offs)]
    y = mxq(f64(w1), 0, "e4m3").T @ xq
    z = relu(y + 0.75) * (f64(cf1)[np.arange(H)[:, None], runs(fn, H)]) + relu(y) * (f64(cf2)[np.arange(H)[:, None], runs(fn, H)]) + relu(y + -0.75) * (f64(cf3)[np.arange(H)[:, None], runs(fn, H)])
    return mxq(f64(w2), 0, "e4m3").T @ mxq(z, 0, "e4m3")

@@ -1,0 +1,260 @@
+from contextlib import ExitStack
+
+import concourse.mybir as mybir
+from concourse.masks import make_identity
+
+F32 = mybir.dt.float32
+BF16 = mybir.dt.bfloat16
+I32 = mybir.dt.int32
+U32 = mybir.dt.uint32
+U16 = mybir.dt.uint16
+U8 = mybir.dt.uint8
+FP8X4 = mybir.dt.float8_e4m3fn_x4
+RELU = mybir.ActivationFunctionType.Relu
+MULT = mybir.AluOpType.mult
+ADD = mybir.AluOpType.add
+
+K, T, S, H, N, U = 512, 2048, 512, 512, 512, 512
+FLOPS = 2 * K * H * S + 2 * H * N * S
+
+P = 128
+PACK = 4
+LANES = 16
+HALF = S // 2
+KNOT = 0.75
+W1_VECTOR_COLUMNS = 80
+
+
+def tile_picked_kan8_none_p_kernel(
+    tc, x_words, x_scales, w1, cf1, cf2, cf3, w2, offs, fn, out
+):
+    nc = tc.nc
+    with ExitStack() as ctx:
+        lists = ctx.enter_context(tc.tile_pool(name="lists", bufs=1))
+        keep = ctx.enter_context(tc.tile_pool(name="keep", bufs=1))
+        ring = ctx.enter_context(tc.tile_pool(name="ring", bufs=12))
+        psum = ctx.enter_context(tc.psum_pool(name="psum", bufs=1))
+
+        def bank(number, shape, name):
+            return psum.tile(shape, F32, name=name, tag="bank%d" % number)
+
+        offs_sb = lists.tile([P, S // LANES], U16, name="offs_sb")
+        fn_sb = lists.tile([P, S // LANES], U16, name="fn_sb")
+        scale_window = keep.tile([P, T], U8, name="scale_window")
+        word_window = keep.tile([P, T], I32, name="word_window")
+        w1_raw = keep.tile([P, PACK, H], F32, name="w1_raw")
+        w2_raw = keep.tile([P, PACK, N], F32, name="w2_raw")
+        tables = [
+            [keep.tile([P, U], F32, name="cf%d_%d" % (k, t)) for k in range(3)]
+            for t in range(PACK)
+        ]
+
+        nc.vector.memset(scale_window[:].bitcast(I32), 0)
+        nc.sync.dma_start(offs_sb[:], offs)
+        nc.sync.dma_start(w1_raw[:], w1.rearrange("(p j) c -> p j c", j=PACK))
+        scale_rows = x_scales[0].bitcast(I32).rearrange("(q r) c -> r q c", r=4)
+        for r in range(4):
+            nc.scalar.dma_start(scale_window[r:P:32, :].bitcast(I32), scale_rows[r])
+        nc.sync.dma_start(word_window[:], x_words[0].rearrange("p n t -> p (n t)").bitcast(I32))
+        nc.sync.dma_start(fn_sb[:], fn)
+
+        def load_tables(t):
+            for k, cf in enumerate((cf1, cf2, cf3)):
+                nc.sync.dma_start(tables[t][k][:], cf.rearrange("(p t) c -> t p c", t=PACK)[t])
+
+        load_tables(0)
+        load_tables(1)
+        nc.sync.dma_start(w2_raw[:], w2.rearrange("(p j) c -> p j c", j=PACK))
+        load_tables(2)
+        load_tables(3)
+
+        minus_knot = keep.tile([P, 1], F32, name="minus_knot")
+        zero = keep.tile([P, 1], F32, name="zero")
+        plus_knot = keep.tile([P, 1], F32, name="plus_knot")
+        nc.vector.memset(minus_knot[:], -KNOT)
+        nc.vector.memset(zero[:], 0.0)
+        nc.scalar.activation(plus_knot[:], minus_knot[:], RELU, bias=zero[:], scale=-1.0)
+        shifts = (plus_knot, zero, minus_knot)
+        identity = keep.tile([P, P], F32, name="identity")
+        make_identity(nc, identity[:])
+
+        w1_bf = keep.tile([P, PACK * H], BF16, name="w1_bf", align_bytes=64)
+        w1_codes = keep.tile([P, H], U32, name="w1_codes", align_bytes=64)
+        w1_scales = keep.tile([P, H], U8, name="w1_scales", align_bytes=64)
+        w1_to = w1_bf[:].rearrange("p (t m j) -> p m t j", t=PACK, j=PACK)
+        w1_from = w1_raw[:].rearrange("p j (m t) -> p m t j", t=PACK)
+        nc.vector.tensor_copy(w1_to[:, :W1_VECTOR_COLUMNS], w1_from[:, :W1_VECTOR_COLUMNS])
+        nc.scalar.copy(w1_to[:, W1_VECTOR_COLUMNS:], w1_from[:, W1_VECTOR_COLUMNS:])
+        nc.vector.quantize_mx(out=w1_codes[:].bitcast(FP8X4), scales=w1_scales[:], in_=w1_bf[:])
+
+        x_scale = keep.tile([P, S], U8, name="x_scale", align_bytes=64)
+        nc.vector.tensor_copy(x_scale[:], scale_window[:].indirect(offs_sb[:]))
+        x_codes = keep.tile([P, S], U32, name="x_codes", align_bytes=64)
+        for h in range(2):
+            nc.vector.tensor_copy(
+                x_codes[:, h * HALF : (h + 1) * HALF],
+                word_window[:].bitcast(U32).indirect(offs_sb[:, h * HALF // LANES : (h + 1) * HALF // LANES]),
+            )
+
+        ramps = [
+            [keep.tile([P, S], F32, name="ramp%d_%d" % (k, t)) for k in range(3)]
+            for t in range(PACK)
+        ]
+
+        def first_product(t, tokens, number):
+            width = tokens.stop - tokens.start
+            y = bank(number, [P, width], "y")
+            features = slice(t * P, (t + 1) * P)
+            nc.tensor.matmul_mx(
+                out=y[:],
+                lhsT=w1_codes[:, features].bitcast(FP8X4),
+                lhsT_scale=w1_scales[:, features],
+                rhs=x_codes[:, tokens].bitcast(FP8X4),
+                rhs_scale=x_scale[:, tokens],
+                start=True,
+                stop=True,
+            )
+            return y
+
+        def ramp(t, k, tokens, y):
+            nc.scalar.activation(ramps[t][k][:, tokens], y[:], RELU, bias=shifts[k][:])
+
+        halves = [slice(0, HALF), slice(HALF, S)]
+        y0 = [first_product(0, halves[h], h) for h in range(2)]
+        for k in range(3):
+            for h in range(2):
+                ramp(0, k, halves[h], y0[h])
+        for t, number in ((1, 2), (2, 3), (3, 0)):
+            y = first_product(t, slice(0, S), number)
+            for k in range(3):
+                ramp(t, k, slice(0, S), y)
+
+        w2_bf = keep.tile([P, PACK * N], BF16, name="w2_bf", tag="before_b", align_bytes=64)
+        w2_codes = keep.tile([P, N], U32, name="w2_codes", align_bytes=64)
+        w2_scales = keep.tile([P, N], U8, name="w2_scales", align_bytes=64)
+
+        def prepare_w2():
+            w2_to = w2_bf[:].rearrange("p (c i j) -> p c j i", i=4, j=PACK)
+            w2_from = w2_raw[:].rearrange("p j (c i) -> p c j i", i=4)
+            for part in range(2):
+                cs = slice(part * 64, (part + 1) * 64)
+                nc.scalar.copy(w2_to[:, cs], w2_from[:, cs])
+            nc.vector.quantize_mx(out=w2_codes[:].bitcast(FP8X4), scales=w2_scales[:], in_=w2_bf[:])
+
+        def product(t, k, tokens, term=None):
+            if term is None:
+                term = ring.tile([P, tokens.stop - tokens.start], F32, name="term")
+            nc.vector.tensor_tensor(
+                term[:],
+                tables[t][k][:].indirect(fn_sb[:, tokens.start // LANES : tokens.stop // LANES]),
+                ramps[t][k][:, tokens],
+                MULT,
+            )
+            return term
+
+        def add_turned(z_turned, e, terms):
+            for b in range(terms[0].shape[1] // P):
+                for k in range(3):
+                    nc.tensor.matmul(
+                        z_turned[:, b, e, :],
+                        terms[k][:, b * P : (b + 1) * P],
+                        identity[:],
+                        start=(k == 0),
+                        stop=(k == 2),
+                        is_transpose=True,
+                    )
+
+        def round_pairs(z_turned, blocks, name, copy):
+            pairs = keep.tile([P, blocks * 2 * P], BF16, name=name)
+            copy(
+                pairs[:].rearrange("s (b p e) -> s b p e", p=P, e=2),
+                z_turned[:].rearrange("s b e p -> s b p e"),
+            )
+            return pairs
+
+        def turn_back(back, u, pairs, first, blocks):
+            for b in range(blocks):
+                words = pairs[:, (first + b) * 2 * P : (first + b + 1) * 2 * P].bitcast(F32)
+                nc.tensor.transpose(back[:, b, u, :], words, identity[:])
+
+        out_view = out.rearrange("(g p) s -> p g s", p=P)
+
+        def weave(back, width, name, tag, copy):
+            z_bf = keep.tile([P, PACK * width], BF16, name="z_bf" + name, tag=tag, align_bytes=64)
+            copy(
+                z_bf[:].bitcast(F32).rearrange("p (b s u) -> p b s u", s=P, u=2),
+                back[:].rearrange("p b u s -> p b s u"),
+            )
+            return z_bf
+
+        def second_product(z_bf, tokens, ways_out, name):
+            width = tokens.stop - tokens.start
+            z_codes = keep.tile([P, width], U32, name="z_codes" + name, align_bytes=64)
+            z_scales = keep.tile([P, width], U8, name="z_scales" + name, align_bytes=64)
+            nc.vector.quantize_mx(out=z_codes[:].bitcast(FP8X4), scales=z_scales[:], in_=z_bf[:])
+            per_bank = PACK // len(ways_out)
+            for i, (number, copy, queue) in enumerate(ways_out):
+                acc = bank(number, [P, per_bank, width], "acc")
+                for g in range(per_bank):
+                    rows = slice((i * per_bank + g) * P, (i * per_bank + g + 1) * P)
+                    nc.tensor.matmul_mx(
+                        out=acc[:, g, :],
+                        lhsT=w2_codes[:, rows].bitcast(FP8X4),
+                        lhsT_scale=w2_scales[:, rows],
+                        rhs=z_codes[:].bitcast(FP8X4),
+                        rhs_scale=z_scales[:],
+                        start=True,
+                        stop=True,
+                    )
+                result = keep.tile([P, per_bank, width], F32, name="result%s_%d" % (name, i))
+                copy(result[:], acc[:])
+                queue.dma_start(out_view[:, i * per_bank : (i + 1) * per_bank, tokens], result[:])
+
+        on_scalar, on_vector = nc.scalar.copy, nc.vector.tensor_copy
+
+        z_low = [bank(4 + h, [P, 2, 2, P], "z_low") for h in range(2)]
+        for t in range(2):
+            terms = [[None] * 3, [None] * 3]
+            for k in range(3):
+                for h in range(2):
+                    terms[h][k] = product(t, k, halves[h])
+            for h in range(2):
+                add_turned(z_low[h], t, terms[h])
+        prepare_w2()
+        pairs_low = [round_pairs(z_low[h], 2, "pairs_low%d" % h, on_scalar) for h in range(2)]
+
+        def upper_slots(tokens, z_bank, back_bank, name, terms_tag, z_tag, copy):
+            width = tokens.stop - tokens.start
+            blocks = width // P
+            back = bank(back_bank, [P, blocks, 2, P], "back")
+            turn_back(back, 0, pairs_low[tokens.start // HALF], tokens.start % HALF // P, blocks)
+            z_high = bank(z_bank, [P, blocks, 2, P], "z_high")
+            terms = keep.tile([P, 2, 3, width], F32, name="terms" + name, tag=terms_tag, align_bytes=64)
+            for e in range(2):
+                add_turned(z_high, e, [product(2 + e, k, tokens, terms[:, e, k, :]) for k in range(3)])
+            pairs_high = round_pairs(z_high, blocks, "pairs_high" + name, copy)
+            turn_back(back, 1, pairs_high, 0, blocks)
+            return weave(back, width, name, z_tag, copy)
+
+        first, second, last = slice(0, 256), slice(256, 384), slice(384, 512)
+        z_first = upper_slots(first, 6, 0, "a", "terms_a", "before_c", on_scalar)
+        z_second = upper_slots(second, 7, 2, "b", "before_b", "z_b", on_scalar)
+        second_product(z_first, first, ((4, on_scalar, nc.sync), (5, on_scalar, nc.sync)), "a")
+        back = bank(3, [P, 1, 2, P], "back")
+        turn_back(back, 0, pairs_low[1], 1, 1)
+        z_last = keep.tile([P, PACK * P], BF16, name="z_last", align_bytes=64)
+        nc.scalar.copy(z_last[:].bitcast(F32).rearrange("p (s u) -> p s u", u=2)[:, :, 0], back[:, 0, 0, :])
+        terms_last = keep.tile([P, 3, 2, P], F32, name="terms_c", tag="before_c", align_bytes=64)
+        partial = keep.tile([P, 2, P], F32, name="partial")
+        for k, e in ((0, 0), (0, 1), (1, 0), (1, 1), (2, 0)):
+            product(2 + e, k, last, terms_last[:, k, e, :])
+        nc.vector.tensor_tensor(partial[:], terms_last[:, 0], terms_last[:, 1], ADD)
+        product(3, 2, last, terms_last[:, 2, 1, :])
+        second_product(z_second, second, ((6, on_scalar, nc.sync),), "b")
+        nc.vector.tensor_tensor(
+            z_last[:].rearrange("p (s u e) -> p s u e", u=2, e=2)[:, :, 1, :],
+            partial[:].rearrange("p e s -> p s e"),
+            terms_last[:, 2].rearrange("p e s -> p s e"),
+            ADD,
+        )
+        second_product(z_last, last, ((7, on_scalar, nc.scalar), (1, on_vector, nc.sync)), "c")

@@ -13,6 +13,7 @@ FP8X4 = mybir.dt.float8_e4m3fn_x4
 RELU = mybir.ActivationFunctionType.Relu
 MULT = mybir.AluOpType.mult
 ADD = mybir.AluOpType.add
+MAX = mybir.AluOpType.max
 
 K, T, S, H, N, U = 512, 2048, 512, 512, 512, 512
 FLOPS = 2 * K * H * S + 2 * H * N * S
@@ -22,7 +23,7 @@ PACK = 4
 LANES = 16
 HALF = S // 2
 KNOT = 0.75
-W1_VECTOR_COLUMNS = 80
+W1_VECTOR_COLUMNS = 64
 
 
 def tile_picked_kan8_none_p_kernel(
@@ -32,41 +33,44 @@ def tile_picked_kan8_none_p_kernel(
     with ExitStack() as ctx:
         lists = ctx.enter_context(tc.tile_pool(name="lists", bufs=1))
         keep = ctx.enter_context(tc.tile_pool(name="keep", bufs=1))
-        ring = ctx.enter_context(tc.tile_pool(name="ring", bufs=12))
         psum = ctx.enter_context(tc.psum_pool(name="psum", bufs=1))
 
         def bank(number, shape, name):
             return psum.tile(shape, F32, name=name, tag="bank%d" % number)
+
+        def wide(t, k):
+            return t < 2
 
         offs_sb = lists.tile([P, S // LANES], U16, name="offs_sb")
         fn_sb = lists.tile([P, S // LANES], U16, name="fn_sb")
         scale_window = keep.tile([P, T], U8, name="scale_window")
         word_window = keep.tile([P, T], I32, name="word_window")
         w1_raw = keep.tile([P, PACK, H], F32, name="w1_raw")
-        w2_raw = keep.tile([P, PACK, N], F32, name="w2_raw")
+        w2_raw = keep.tile([P, PACK, N], F32, name="w2_raw", tag="w2_then_pairs")
         tables = [
-            [keep.tile([P, U], F32, name="cf%d_%d" % (k, t)) for k in range(3)]
+            [keep.tile([P, 2 * U if wide(t, k) else U], F32, name="cf%d_%d" % (k, t)) for k in range(3)]
             for t in range(PACK)
         ]
 
-        nc.vector.memset(scale_window[:].bitcast(I32), 0)
+        nc.gpsimd.memset(scale_window[:].bitcast(I32), 0)
+        def load_table(t, k):
+            cf = (cf1, cf2, cf3)[k]
+            nc.sync.dma_start(tables[t][k][:, :U], cf.rearrange("(p t) c -> t p c", t=PACK)[t])
+
+        nc.sync.dma_start(fn_sb[:], fn)
+        load_table(0, 1)
         nc.sync.dma_start(offs_sb[:], offs)
-        nc.sync.dma_start(w1_raw[:], w1.rearrange("(p j) c -> p j c", j=PACK))
         scale_rows = x_scales[0].bitcast(I32).rearrange("(q r) c -> r q c", r=4)
         for r in range(4):
-            nc.scalar.dma_start(scale_window[r:P:32, :].bitcast(I32), scale_rows[r])
+            nc.sync.dma_start(scale_window[r:P:32, :].bitcast(I32), scale_rows[r])
+        nc.sync.dma_start(w1_raw[:], w1.rearrange("(p j) c -> p j c", j=PACK))
         nc.sync.dma_start(word_window[:], x_words[0].rearrange("p n t -> p (n t)").bitcast(I32))
-        nc.sync.dma_start(fn_sb[:], fn)
-
-        def load_tables(t):
-            for k, cf in enumerate((cf1, cf2, cf3)):
-                nc.sync.dma_start(tables[t][k][:], cf.rearrange("(p t) c -> t p c", t=PACK)[t])
-
-        load_tables(0)
-        load_tables(1)
+        for t, k in ((1, 1), (0, 0), (1, 0), (0, 2), (1, 2)):
+            load_table(t, k)
         nc.sync.dma_start(w2_raw[:], w2.rearrange("(p j) c -> p j c", j=PACK))
-        load_tables(2)
-        load_tables(3)
+        for t in (2, 3):
+            for k in range(3):
+                load_table(t, k)
 
         minus_knot = keep.tile([P, 1], F32, name="minus_knot")
         zero = keep.tile([P, 1], F32, name="zero")
@@ -78,6 +82,14 @@ def tile_picked_kan8_none_p_kernel(
         identity = keep.tile([P, P], F32, name="identity")
         make_identity(nc, identity[:])
 
+        slopes = keep.tile([P, 2, S], F32, name="slopes")
+        middle = keep.tile([P, 2, S], F32, name="middle")
+
+        def fetch_slopes(t):
+            nc.vector.tensor_copy(slopes[:, t, :], tables[t][1][:].indirect(fn_sb[:]))
+
+        fetch_slopes(0)
+
         w1_bf = keep.tile([P, PACK * H], BF16, name="w1_bf", align_bytes=64)
         w1_codes = keep.tile([P, H], U32, name="w1_codes", align_bytes=64)
         w1_scales = keep.tile([P, H], U8, name="w1_scales", align_bytes=64)
@@ -85,49 +97,50 @@ def tile_picked_kan8_none_p_kernel(
         w1_from = w1_raw[:].rearrange("p j (m t) -> p m t j", t=PACK)
         nc.vector.tensor_copy(w1_to[:, :W1_VECTOR_COLUMNS], w1_from[:, :W1_VECTOR_COLUMNS])
         nc.scalar.copy(w1_to[:, W1_VECTOR_COLUMNS:], w1_from[:, W1_VECTOR_COLUMNS:])
-        nc.vector.quantize_mx(out=w1_codes[:].bitcast(FP8X4), scales=w1_scales[:], in_=w1_bf[:])
 
         x_scale = keep.tile([P, S], U8, name="x_scale", align_bytes=64)
         nc.vector.tensor_copy(x_scale[:], scale_window[:].indirect(offs_sb[:]))
-        x_codes = keep.tile([P, S], U32, name="x_codes", align_bytes=64)
-        for h in range(2):
-            nc.vector.tensor_copy(
-                x_codes[:, h * HALF : (h + 1) * HALF],
-                word_window[:].bitcast(U32).indirect(offs_sb[:, h * HALF // LANES : (h + 1) * HALF // LANES]),
-            )
+        nc.vector.quantize_mx(out=w1_codes[:].bitcast(FP8X4), scales=w1_scales[:], in_=w1_bf[:])
+        halves = [slice(0, HALF), slice(HALF, S)]
+        x_codes = [keep.tile([P, HALF], U32, name="x_codes%d" % h, align_bytes=64) for h in range(2)]
 
-        ramps = [
-            [keep.tile([P, S], F32, name="ramp%d_%d" % (k, t)) for k in range(3)]
-            for t in range(PACK)
-        ]
-
-        def first_product(t, tokens, number):
-            width = tokens.stop - tokens.start
-            y = bank(number, [P, width], "y")
+        def first_product(y, t, h):
             features = slice(t * P, (t + 1) * P)
             nc.tensor.matmul_mx(
-                out=y[:],
+                out=y,
                 lhsT=w1_codes[:, features].bitcast(FP8X4),
                 lhsT_scale=w1_scales[:, features],
-                rhs=x_codes[:, tokens].bitcast(FP8X4),
-                rhs_scale=x_scale[:, tokens],
+                rhs=x_codes[h][:].bitcast(FP8X4),
+                rhs_scale=x_scale[:, halves[h]],
                 start=True,
                 stop=True,
             )
-            return y
 
-        def ramp(t, k, tokens, y):
-            nc.scalar.activation(ramps[t][k][:, tokens], y[:], RELU, bias=shifts[k][:])
-
-        halves = [slice(0, HALF), slice(HALF, S)]
-        y0 = [first_product(0, halves[h], h) for h in range(2)]
-        for k in range(3):
+        y_low = [bank(h, [P, 2, HALF], "y_low") for h in range(2)]
+        y_high = [bank(2 + e, [P, S], "y_high") for e in range(2)]
+        for h in range(2):
+            nc.vector.tensor_copy(
+                x_codes[h][:],
+                word_window[:].bitcast(U32).indirect(offs_sb[:, h * HALF // LANES : (h + 1) * HALF // LANES]),
+            )
+            for t in range(2):
+                first_product(y_low[h][:, t, :], t, h)
+        for e in range(2):
             for h in range(2):
-                ramp(0, k, halves[h], y0[h])
-        for t, number in ((1, 2), (2, 3), (3, 0)):
-            y = first_product(t, slice(0, S), number)
+                first_product(y_high[e][:, halves[h]], 2 + e, h)
+
+        ramps = [keep.tile([P, PACK, S], F32, name="ramps%d" % k) for k in range(3)]
+        fetch_slopes(1)
+        for h in range(2):
+            nc.scalar.activation(ramps[0][:, 0:2, halves[h]], y_low[h][:], RELU, bias=shifts[0][:])
+            nc.vector.scalar_tensor_tensor(
+                middle[:, :, halves[h]], y_low[h][:], 0.0, slopes[:, :, halves[h]], MAX, MULT
+            )
+        for h in range(2):
+            nc.scalar.activation(ramps[2][:, 0:2, halves[h]], y_low[h][:], RELU, bias=shifts[2][:])
+        for t in (2, 3):
             for k in range(3):
-                ramp(t, k, slice(0, S), y)
+                nc.scalar.activation(ramps[k][:, t, :], y_high[t - 2][:], RELU, bias=shifts[k][:])
 
         w2_bf = keep.tile([P, PACK * N], BF16, name="w2_bf", tag="before_b", align_bytes=64)
         w2_codes = keep.tile([P, N], U32, name="w2_codes", align_bytes=64)
@@ -141,13 +154,11 @@ def tile_picked_kan8_none_p_kernel(
                 nc.scalar.copy(w2_to[:, cs], w2_from[:, cs])
             nc.vector.quantize_mx(out=w2_codes[:].bitcast(FP8X4), scales=w2_scales[:], in_=w2_bf[:])
 
-        def product(t, k, tokens, term=None):
-            if term is None:
-                term = ring.tile([P, tokens.stop - tokens.start], F32, name="term")
+        def product(t, k, tokens, term):
             nc.vector.tensor_tensor(
-                term[:],
+                term,
                 tables[t][k][:].indirect(fn_sb[:, tokens.start // LANES : tokens.stop // LANES]),
-                ramps[t][k][:, tokens],
+                ramps[k][:, t, tokens],
                 MULT,
             )
             return term
@@ -164,13 +175,11 @@ def tile_picked_kan8_none_p_kernel(
                         is_transpose=True,
                     )
 
-        def round_pairs(z_turned, blocks, name, copy):
-            pairs = keep.tile([P, blocks * 2 * P], BF16, name=name)
-            copy(
-                pairs[:].rearrange("s (b p e) -> s b p e", p=P, e=2),
+        def round_pairs(z_turned, pairs):
+            nc.scalar.copy(
+                pairs.rearrange("s (b p e) -> s b p e", p=P, e=2),
                 z_turned[:].rearrange("s b e p -> s b p e"),
             )
-            return pairs
 
         def turn_back(back, u, pairs, first, blocks):
             for b in range(blocks):
@@ -213,35 +222,51 @@ def tile_picked_kan8_none_p_kernel(
         on_scalar, on_vector = nc.scalar.copy, nc.vector.tensor_copy
 
         z_low = [bank(4 + h, [P, 2, 2, P], "z_low") for h in range(2)]
+        outer_low = keep.tile([P, 2, 2, S], F32, name="outer_low")
         for t in range(2):
-            terms = [[None] * 3, [None] * 3]
-            for k in range(3):
-                for h in range(2):
-                    terms[h][k] = product(t, k, halves[h])
+            product(t, 0, slice(0, S), outer_low[:, t, 0, :])
+        for t in range(2):
+            product(t, 2, slice(0, S), outer_low[:, t, 1, :])
             for h in range(2):
-                add_turned(z_low[h], t, terms[h])
+                add_turned(
+                    z_low[h], t, [middle[:, t, halves[h]], outer_low[:, t, 0, halves[h]], outer_low[:, t, 1, halves[h]]]
+                )
         prepare_w2()
-        pairs_low = [round_pairs(z_low[h], 2, "pairs_low%d" % h, on_scalar) for h in range(2)]
+        pairs_low = keep.tile([P, S * 2], BF16, name="pairs_low", tag="w2_then_pairs")
+        for h in range(2):
+            round_pairs(z_low[h], pairs_low[:, h * S : (h + 1) * S])
 
-        def upper_slots(tokens, z_bank, back_bank, name, terms_tag, z_tag, copy):
+        def upper_slots(tokens, z_banks, back_bank, name, terms_tag, z_tag):
             width = tokens.stop - tokens.start
             blocks = width // P
             back = bank(back_bank, [P, blocks, 2, P], "back")
-            turn_back(back, 0, pairs_low[tokens.start // HALF], tokens.start % HALF // P, blocks)
-            z_high = bank(z_bank, [P, blocks, 2, P], "z_high")
+            turn_back(back, 0, pairs_low, tokens.start // P, blocks)
+            z_high = [bank(number, [P, 1, 2, P], "z_high") for number in z_banks]
             terms = keep.tile([P, 2, 3, width], F32, name="terms" + name, tag=terms_tag, align_bytes=64)
             for e in range(2):
-                add_turned(z_high, e, [product(2 + e, k, tokens, terms[:, e, k, :]) for k in range(3)])
-            pairs_high = round_pairs(z_high, blocks, "pairs_high" + name, copy)
+                for k in range(3):
+                    product(2 + e, k, tokens, terms[:, e, k, :])
+                    for b in range(blocks):
+                        nc.tensor.matmul(
+                            z_high[b][:, 0, e, :],
+                            terms[:, e, k, b * P : (b + 1) * P],
+                            identity[:],
+                            start=(k == 0),
+                            stop=(k == 2),
+                            is_transpose=True,
+                        )
+            pairs_high = keep.tile([P, width * 2], BF16, name="pairs_high" + name)
+            for b in range(blocks):
+                round_pairs(z_high[b], pairs_high[:, b * 2 * P : (b + 1) * 2 * P])
             turn_back(back, 1, pairs_high, 0, blocks)
-            return weave(back, width, name, z_tag, copy)
+            return weave(back, width, name, z_tag, on_scalar)
 
         first, second, last = slice(0, 256), slice(256, 384), slice(384, 512)
-        z_first = upper_slots(first, 6, 0, "a", "terms_a", "before_c", on_scalar)
-        z_second = upper_slots(second, 7, 2, "b", "before_b", "z_b", on_scalar)
+        z_first = upper_slots(first, (6, 3), 0, "a", "terms_a", "before_c")
+        z_second = upper_slots(second, (7,), 1, "b", "before_b", "z_b")
         second_product(z_first, first, ((4, on_scalar, nc.sync), (5, on_scalar, nc.sync)), "a")
-        back = bank(3, [P, 1, 2, P], "back")
-        turn_back(back, 0, pairs_low[1], 1, 1)
+        back = bank(2, [P, 1, 2, P], "back")
+        turn_back(back, 0, pairs_low, 3, 1)
         z_last = keep.tile([P, PACK * P], BF16, name="z_last", align_bytes=64)
         nc.scalar.copy(z_last[:].bitcast(F32).rearrange("p (s u) -> p s u", u=2)[:, :, 0], back[:, 0, 0, :])
         terms_last = keep.tile([P, 3, 2, P], F32, name="terms_c", tag="before_c", align_bytes=64)
@@ -257,4 +282,4 @@ def tile_picked_kan8_none_p_kernel(
             terms_last[:, 2].rearrange("p e s -> p s e"),
             ADD,
         )
-        second_product(z_last, last, ((7, on_scalar, nc.scalar), (1, on_vector, nc.sync)), "c")
+        second_product(z_last, last, ((7, on_scalar, nc.scalar), (3, on_vector, nc.sync)), "c")

@@ -23,7 +23,7 @@ PACK = 4
 LANES = 16
 HALF = S // 2
 KNOT = 0.75
-W1_VECTOR_COLUMNS = 64
+W1_VECTOR_COLUMNS = 72
 
 
 def tile_picked_kan8_none_p_kernel(
@@ -52,7 +52,7 @@ def tile_picked_kan8_none_p_kernel(
             for t in range(PACK)
         ]
 
-        nc.gpsimd.memset(scale_window[:].bitcast(I32), 0)
+        nc.vector.memset(scale_window[:].bitcast(I32), 0)
         def load_table(t, k):
             cf = (cf1, cf2, cf3)[k]
             nc.sync.dma_start(tables[t][k][:, :U], cf.rearrange("(p t) c -> t p c", t=PACK)[t])
@@ -63,9 +63,10 @@ def tile_picked_kan8_none_p_kernel(
         scale_rows = x_scales[0].bitcast(I32).rearrange("(q r) c -> r q c", r=4)
         for r in range(4):
             nc.sync.dma_start(scale_window[r:P:32, :].bitcast(I32), scale_rows[r])
+        load_table(1, 1)
         nc.sync.dma_start(w1_raw[:], w1.rearrange("(p j) c -> p j c", j=PACK))
         nc.sync.dma_start(word_window[:], x_words[0].rearrange("p n t -> p (n t)").bitcast(I32))
-        for t, k in ((1, 1), (0, 0), (1, 0), (0, 2), (1, 2)):
+        for t, k in ((1, 0), (1, 2), (0, 0), (0, 2)):
             load_table(t, k)
         nc.sync.dma_start(w2_raw[:], w2.rearrange("(p j) c -> p j c", j=PACK))
         for t in (2, 3):
@@ -83,12 +84,8 @@ def tile_picked_kan8_none_p_kernel(
         make_identity(nc, identity[:])
 
         slopes = keep.tile([P, 2, S], F32, name="slopes")
-        middle = keep.tile([P, 2, S], F32, name="middle")
-
-        def fetch_slopes(t):
+        for t in range(2):
             nc.vector.tensor_copy(slopes[:, t, :], tables[t][1][:].indirect(fn_sb[:]))
-
-        fetch_slopes(0)
 
         w1_bf = keep.tile([P, PACK * H], BF16, name="w1_bf", align_bytes=64)
         w1_codes = keep.tile([P, H], U32, name="w1_codes", align_bytes=64)
@@ -116,28 +113,38 @@ def tile_picked_kan8_none_p_kernel(
                 stop=True,
             )
 
-        y_low = [bank(h, [P, 2, HALF], "y_low") for h in range(2)]
-        y_high = [bank(2 + e, [P, S], "y_high") for e in range(2)]
+        y_low = [[bank(2 * h + t, [P, HALF], "y_low") for t in range(2)] for h in range(2)]
+        y_high = [bank(6 + e, [P, S], "y_high") for e in range(2)]
         for h in range(2):
             nc.vector.tensor_copy(
                 x_codes[h][:],
                 word_window[:].bitcast(U32).indirect(offs_sb[:, h * HALF // LANES : (h + 1) * HALF // LANES]),
             )
             for t in range(2):
-                first_product(y_low[h][:, t, :], t, h)
+                first_product(y_low[h][t][:], t, h)
         for e in range(2):
             for h in range(2):
                 first_product(y_high[e][:, halves[h]], 2 + e, h)
 
         ramps = [keep.tile([P, PACK, S], F32, name="ramps%d" % k) for k in range(3)]
-        fetch_slopes(1)
-        for h in range(2):
-            nc.scalar.activation(ramps[0][:, 0:2, halves[h]], y_low[h][:], RELU, bias=shifts[0][:])
+        terms_low = keep.tile([P, 2, 3, S], F32, name="terms_low")
+
+        def middle_term(t, h):
             nc.vector.scalar_tensor_tensor(
-                middle[:, :, halves[h]], y_low[h][:], 0.0, slopes[:, :, halves[h]], MAX, MULT
+                terms_low[:, t, 1, halves[h]], y_low[h][t][:], 0.0, slopes[:, t, halves[h]], MAX, MULT
             )
+
+        def ramp_low(t, k, h):
+            nc.scalar.activation(ramps[k][:, t, halves[h]], y_low[h][t][:], RELU, bias=shifts[k][:])
+
         for h in range(2):
-            nc.scalar.activation(ramps[2][:, 0:2, halves[h]], y_low[h][:], RELU, bias=shifts[2][:])
+            middle_term(0, h)
+            ramp_low(1, 0, h)
+        for h in range(2):
+            middle_term(1, h)
+        for t, k in ((1, 2), (0, 0), (0, 2)):
+            for h in range(2):
+                ramp_low(t, k, h)
         for t in (2, 3):
             for k in range(3):
                 nc.scalar.activation(ramps[k][:, t, :], y_high[t - 2][:], RELU, bias=shifts[k][:])
@@ -188,14 +195,6 @@ def tile_picked_kan8_none_p_kernel(
 
         out_view = out.rearrange("(g p) s -> p g s", p=P)
 
-        def weave(back, width, name, tag, copy):
-            z_bf = keep.tile([P, PACK * width], BF16, name="z_bf" + name, tag=tag, align_bytes=64)
-            copy(
-                z_bf[:].bitcast(F32).rearrange("p (b s u) -> p b s u", s=P, u=2),
-                back[:].rearrange("p b u s -> p b s u"),
-            )
-            return z_bf
-
         def second_product(z_bf, tokens, ways_out, name):
             width = tokens.stop - tokens.start
             z_codes = keep.tile([P, width], U32, name="z_codes" + name, align_bytes=64)
@@ -222,25 +221,25 @@ def tile_picked_kan8_none_p_kernel(
         on_scalar, on_vector = nc.scalar.copy, nc.vector.tensor_copy
 
         z_low = [bank(4 + h, [P, 2, 2, P], "z_low") for h in range(2)]
-        outer_low = keep.tile([P, 2, 2, S], F32, name="outer_low")
-        for t in range(2):
-            product(t, 0, slice(0, S), outer_low[:, t, 0, :])
-        for t in range(2):
-            product(t, 2, slice(0, S), outer_low[:, t, 1, :])
-            for h in range(2):
-                add_turned(
-                    z_low[h], t, [middle[:, t, halves[h]], outer_low[:, t, 0, halves[h]], outer_low[:, t, 1, halves[h]]]
-                )
+        product(1, 0, slice(0, S), terms_low[:, 1, 0, :])
+        product(1, 2, slice(0, S), terms_low[:, 1, 2, :])
+        for h in range(2):
+            add_turned(z_low[h], 1, [terms_low[:, 1, k, halves[h]] for k in range(3)])
+        for k in (0, 2):
+            product(0, k, slice(0, S), terms_low[:, 0, k, :])
+        for h in range(2):
+            add_turned(z_low[h], 0, [terms_low[:, 0, k, halves[h]] for k in (1, 0, 2)])
         prepare_w2()
         pairs_low = keep.tile([P, S * 2], BF16, name="pairs_low", tag="w2_then_pairs")
         for h in range(2):
             round_pairs(z_low[h], pairs_low[:, h * S : (h + 1) * S])
 
-        def upper_slots(tokens, z_banks, back_bank, name, terms_tag, z_tag):
+        def upper_slots(tokens, z_banks, back_banks, name, terms_tag, z_tag):
             width = tokens.stop - tokens.start
             blocks = width // P
-            back = bank(back_bank, [P, blocks, 2, P], "back")
-            turn_back(back, 0, pairs_low, tokens.start // P, blocks)
+            back = [bank(number, [P, 1, 2, P], "back") for number in back_banks]
+            for b in range(blocks):
+                turn_back(back[b], 0, pairs_low, tokens.start // P + b, 1)
             z_high = [bank(number, [P, 1, 2, P], "z_high") for number in z_banks]
             terms = keep.tile([P, 2, 3, width], F32, name="terms" + name, tag=terms_tag, align_bytes=64)
             for e in range(2):
@@ -256,16 +255,22 @@ def tile_picked_kan8_none_p_kernel(
                             is_transpose=True,
                         )
             pairs_high = keep.tile([P, width * 2], BF16, name="pairs_high" + name)
+            z_bf = keep.tile([P, PACK * width], BF16, name="z_bf" + name, tag=z_tag, align_bytes=64)
             for b in range(blocks):
                 round_pairs(z_high[b], pairs_high[:, b * 2 * P : (b + 1) * 2 * P])
-            turn_back(back, 1, pairs_high, 0, blocks)
-            return weave(back, width, name, z_tag, on_scalar)
+                turn_back(back[b], 1, pairs_high, b, 1)
+            for b in range(blocks):
+                nc.scalar.copy(
+                    z_bf[:, b * PACK * P : (b + 1) * PACK * P].bitcast(F32).rearrange("p (s u) -> p s u", u=2),
+                    back[b][:, 0].rearrange("p u s -> p s u"),
+                )
+            return z_bf
 
         first, second, last = slice(0, 256), slice(256, 384), slice(384, 512)
-        z_first = upper_slots(first, (6, 3), 0, "a", "terms_a", "before_c")
-        z_second = upper_slots(second, (7,), 1, "b", "before_b", "z_b")
-        second_product(z_first, first, ((4, on_scalar, nc.sync), (5, on_scalar, nc.sync)), "a")
-        back = bank(2, [P, 1, 2, P], "back")
+        z_first = upper_slots(first, (2, 3), (0, 4), "a", "terms_a", "before_c")
+        z_second = upper_slots(second, (7,), (1,), "b", "before_b", "z_b")
+        second_product(z_first, first, ((5, on_scalar, nc.sync), (4, on_scalar, nc.sync)), "a")
+        back = bank(6, [P, 1, 2, P], "back")
         turn_back(back, 0, pairs_low, 3, 1)
         z_last = keep.tile([P, PACK * P], BF16, name="z_last", align_bytes=64)
         nc.scalar.copy(z_last[:].bitcast(F32).rearrange("p (s u) -> p s u", u=2)[:, :, 0], back[:, 0, 0, :])
@@ -282,4 +287,4 @@ def tile_picked_kan8_none_p_kernel(
             terms_last[:, 2].rearrange("p e s -> p s e"),
             ADD,
         )
-        second_product(z_last, last, ((7, on_scalar, nc.scalar), (3, on_vector, nc.sync)), "c")
+        second_product(z_last, last, ((3, on_vector, nc.sync), (7, on_scalar, nc.scalar)), "c")

@@ -20,10 +20,12 @@ FLOPS = 2 * K * H * S + 2 * H * N * S
 
 P = 128
 PACK = 4
-LANES = 16
+GROUP = 16
+QUADRANT = 32
+KNOTS = 3
+KNOT_DISTANCE = 0.75
 HALF = S // 2
-KNOT = 0.75
-W1_VECTOR_COLUMNS = 72
+W1_GROUPS_ON_VECTOR = 72
 
 
 def tile_picked_kan8_none_p_kernel(
@@ -38,67 +40,75 @@ def tile_picked_kan8_none_p_kernel(
         def bank(number, shape, name):
             return psum.tile(shape, F32, name=name, tag="bank%d" % number)
 
-        def wide(t, k):
-            return t < 2
+        def entries(list_tile, tokens):
+            return list_tile[:, tokens.start // GROUP : tokens.stop // GROUP]
 
-        offs_sb = lists.tile([P, S // LANES], U16, name="offs_sb")
-        fn_sb = lists.tile([P, S // LANES], U16, name="fn_sb")
+        all_tokens = slice(0, S)
+        halves = [slice(0, HALF), slice(HALF, S)]
+        low_slots, high_slots = (0, 1), (2, 3)
+        middle_knot, outer_knots = 1, (0, 2)
+
+        offs_sb = lists.tile([P, S // GROUP], U16, name="offs_sb")
+        fn_sb = lists.tile([P, S // GROUP], U16, name="fn_sb")
         scale_window = keep.tile([P, T], U8, name="scale_window")
         word_window = keep.tile([P, T], I32, name="word_window")
         w1_raw = keep.tile([P, PACK, H], F32, name="w1_raw")
-        w2_raw = keep.tile([P, PACK, N], F32, name="w2_raw", tag="w2_then_pairs")
+        w2_raw = keep.tile([P, PACK, N], F32, name="w2_raw", tag="w2_raw_then_pairs")
         tables = [
-            [keep.tile([P, 2 * U if wide(t, k) else U], F32, name="cf%d_%d" % (k, t)) for k in range(3)]
+            [
+                keep.tile([P, 2 * U if t in low_slots else U], F32, name="cf%d_%d" % (knot, t))
+                for knot in range(KNOTS)
+            ]
             for t in range(PACK)
         ]
 
-        nc.vector.memset(scale_window[:].bitcast(I32), 0)
-        def load_table(t, k):
-            cf = (cf1, cf2, cf3)[k]
-            nc.sync.dma_start(tables[t][k][:, :U], cf.rearrange("(p t) c -> t p c", t=PACK)[t])
+        def load_table(t, knot):
+            rows = (cf1, cf2, cf3)[knot].rearrange("(p t) c -> t p c", t=PACK)[t]
+            nc.sync.dma_start(tables[t][knot][:, :U], rows)
 
+        nc.vector.memset(scale_window[:].bitcast(I32), 0)
         nc.sync.dma_start(fn_sb[:], fn)
-        load_table(0, 1)
+        load_table(0, middle_knot)
         nc.sync.dma_start(offs_sb[:], offs)
-        scale_rows = x_scales[0].bitcast(I32).rearrange("(q r) c -> r q c", r=4)
-        for r in range(4):
-            nc.sync.dma_start(scale_window[r:P:32, :].bitcast(I32), scale_rows[r])
-        load_table(1, 1)
+        scale_rows = x_scales[0].bitcast(I32).rearrange("(q r) c -> r q c", q=P // QUADRANT)
+        for r in range(QUADRANT // 8):
+            nc.sync.dma_start(scale_window[r:P:QUADRANT, :].bitcast(I32), scale_rows[r])
+        load_table(1, middle_knot)
         nc.sync.dma_start(w1_raw[:], w1.rearrange("(p j) c -> p j c", j=PACK))
         nc.sync.dma_start(word_window[:], x_words[0].rearrange("p n t -> p (n t)").bitcast(I32))
-        for t, k in ((1, 0), (1, 2), (0, 0), (0, 2)):
-            load_table(t, k)
+        for t in low_slots:
+            for knot in outer_knots:
+                load_table(t, knot)
         nc.sync.dma_start(w2_raw[:], w2.rearrange("(p j) c -> p j c", j=PACK))
-        for t in (2, 3):
-            for k in range(3):
-                load_table(t, k)
+        for t in high_slots:
+            for knot in range(KNOTS):
+                load_table(t, knot)
 
-        minus_knot = keep.tile([P, 1], F32, name="minus_knot")
-        zero = keep.tile([P, 1], F32, name="zero")
-        plus_knot = keep.tile([P, 1], F32, name="plus_knot")
-        nc.vector.memset(minus_knot[:], -KNOT)
-        nc.vector.memset(zero[:], 0.0)
-        nc.scalar.activation(plus_knot[:], minus_knot[:], RELU, bias=zero[:], scale=-1.0)
-        shifts = (plus_knot, zero, minus_knot)
+        shift_down = keep.tile([P, 1], F32, name="shift_down")
+        shift_none = keep.tile([P, 1], F32, name="shift_none")
+        shift_up = keep.tile([P, 1], F32, name="shift_up")
+        nc.vector.memset(shift_down[:], -KNOT_DISTANCE)
+        nc.vector.memset(shift_none[:], 0.0)
+        nc.scalar.activation(shift_up[:], shift_down[:], RELU, bias=shift_none[:], scale=-1.0)
+        shifts = (shift_up, shift_none, shift_down)
         identity = keep.tile([P, P], F32, name="identity")
         make_identity(nc, identity[:])
 
-        slopes = keep.tile([P, 2, S], F32, name="slopes")
-        for t in range(2):
-            nc.vector.tensor_copy(slopes[:, t, :], tables[t][1][:].indirect(fn_sb[:]))
+        early_slopes = keep.tile([P, len(low_slots), S], F32, name="early_slopes")
+        for t in low_slots:
+            nc.vector.tensor_copy(early_slopes[:, t, :], tables[t][middle_knot][:].indirect(fn_sb[:]))
 
         w1_bf = keep.tile([P, PACK * H], BF16, name="w1_bf", align_bytes=64)
         w1_codes = keep.tile([P, H], U32, name="w1_codes", align_bytes=64)
         w1_scales = keep.tile([P, H], U8, name="w1_scales", align_bytes=64)
         w1_to = w1_bf[:].rearrange("p (t m j) -> p m t j", t=PACK, j=PACK)
         w1_from = w1_raw[:].rearrange("p j (m t) -> p m t j", t=PACK)
-        nc.vector.tensor_copy(w1_to[:, :W1_VECTOR_COLUMNS], w1_from[:, :W1_VECTOR_COLUMNS])
-        nc.scalar.copy(w1_to[:, W1_VECTOR_COLUMNS:], w1_from[:, W1_VECTOR_COLUMNS:])
+        nc.vector.tensor_copy(w1_to[:, :W1_GROUPS_ON_VECTOR], w1_from[:, :W1_GROUPS_ON_VECTOR])
+        nc.scalar.copy(w1_to[:, W1_GROUPS_ON_VECTOR:], w1_from[:, W1_GROUPS_ON_VECTOR:])
 
         x_scale = keep.tile([P, S], U8, name="x_scale", align_bytes=64)
         nc.vector.tensor_copy(x_scale[:], scale_window[:].indirect(offs_sb[:]))
         nc.vector.quantize_mx(out=w1_codes[:].bitcast(FP8X4), scales=w1_scales[:], in_=w1_bf[:])
-        halves = [slice(0, HALF), slice(HALF, S)]
         x_codes = [keep.tile([P, HALF], U32, name="x_codes%d" % h, align_bytes=64) for h in range(2)]
 
         def first_product(y, t, h):
@@ -113,98 +123,69 @@ def tile_picked_kan8_none_p_kernel(
                 stop=True,
             )
 
-        y_low = [[bank(2 * h + t, [P, HALF], "y_low") for t in range(2)] for h in range(2)]
+        y_low = [[bank(2 * h + t, [P, HALF], "y_low") for t in low_slots] for h in range(2)]
         y_high = [bank(6 + e, [P, S], "y_high") for e in range(2)]
         for h in range(2):
-            nc.vector.tensor_copy(
-                x_codes[h][:],
-                word_window[:].bitcast(U32).indirect(offs_sb[:, h * HALF // LANES : (h + 1) * HALF // LANES]),
-            )
-            for t in range(2):
+            nc.vector.tensor_copy(x_codes[h][:], word_window[:].bitcast(U32).indirect(entries(offs_sb, halves[h])))
+            for t in low_slots:
                 first_product(y_low[h][t][:], t, h)
-        for e in range(2):
+        for e, t in enumerate(high_slots):
             for h in range(2):
-                first_product(y_high[e][:, halves[h]], 2 + e, h)
+                first_product(y_high[e][:, halves[h]], t, h)
 
-        ramps = [keep.tile([P, PACK, S], F32, name="ramps%d" % k) for k in range(3)]
-        terms_low = keep.tile([P, 2, 3, S], F32, name="terms_low")
-
-        def middle_term(t, h):
-            nc.vector.scalar_tensor_tensor(
-                terms_low[:, t, 1, halves[h]], y_low[h][t][:], 0.0, slopes[:, t, halves[h]], MAX, MULT
-            )
-
-        def ramp_low(t, k, h):
-            nc.scalar.activation(ramps[k][:, t, halves[h]], y_low[h][t][:], RELU, bias=shifts[k][:])
-
+        ramps = [keep.tile([P, PACK, S], F32, name="ramps%d" % knot) for knot in range(KNOTS)]
+        terms_low = keep.tile([P, len(low_slots), KNOTS, S], F32, name="terms_low")
         for h in range(2):
-            middle_term(0, h)
-            ramp_low(1, 0, h)
-        for h in range(2):
-            middle_term(1, h)
-        for t, k in ((1, 2), (0, 0), (0, 2)):
+            for t in low_slots:
+                nc.vector.scalar_tensor_tensor(
+                    terms_low[:, t, middle_knot, halves[h]],
+                    y_low[h][t][:],
+                    0.0,
+                    early_slopes[:, t, halves[h]],
+                    MAX,
+                    MULT,
+                )
+        for t in low_slots:
             for h in range(2):
-                ramp_low(t, k, h)
-        for t in (2, 3):
-            for k in range(3):
-                nc.scalar.activation(ramps[k][:, t, :], y_high[t - 2][:], RELU, bias=shifts[k][:])
+                for knot in outer_knots:
+                    nc.scalar.activation(ramps[knot][:, t, halves[h]], y_low[h][t][:], RELU, bias=shifts[knot][:])
+        for e, t in enumerate(high_slots):
+            for knot in range(KNOTS):
+                nc.scalar.activation(ramps[knot][:, t, :], y_high[e][:], RELU, bias=shifts[knot][:])
 
-        w2_bf = keep.tile([P, PACK * N], BF16, name="w2_bf", tag="before_b", align_bytes=64)
+        w2_bf = keep.tile([P, PACK * N], BF16, name="w2_bf", tag="w2_bf_then_terms", align_bytes=64)
         w2_codes = keep.tile([P, N], U32, name="w2_codes", align_bytes=64)
         w2_scales = keep.tile([P, N], U8, name="w2_scales", align_bytes=64)
 
-        def prepare_w2():
-            w2_to = w2_bf[:].rearrange("p (c i j) -> p c j i", i=4, j=PACK)
-            w2_from = w2_raw[:].rearrange("p j (c i) -> p c j i", i=4)
-            for part in range(2):
-                cs = slice(part * 64, (part + 1) * 64)
-                nc.scalar.copy(w2_to[:, cs], w2_from[:, cs])
-            nc.vector.quantize_mx(out=w2_codes[:].bitcast(FP8X4), scales=w2_scales[:], in_=w2_bf[:])
+        def make_term(term, t, knot, tokens):
+            window = tables[t][knot][:].indirect(entries(fn_sb, tokens))
+            nc.vector.tensor_tensor(term, window, ramps[knot][:, t, tokens], MULT)
 
-        def product(t, k, tokens, term):
-            nc.vector.tensor_tensor(
-                term,
-                tables[t][k][:].indirect(fn_sb[:, tokens.start // LANES : tokens.stop // LANES]),
-                ramps[k][:, t, tokens],
-                MULT,
-            )
-            return term
+        def add_turned(z_turned, term, first, last):
+            nc.tensor.matmul(z_turned, term, identity[:], start=first, stop=last, is_transpose=True)
 
-        def add_turned(z_turned, e, terms):
-            for b in range(terms[0].shape[1] // P):
-                for k in range(3):
-                    nc.tensor.matmul(
-                        z_turned[:, b, e, :],
-                        terms[k][:, b * P : (b + 1) * P],
-                        identity[:],
-                        start=(k == 0),
-                        stop=(k == 2),
-                        is_transpose=True,
-                    )
-
-        def round_pairs(z_turned, pairs):
+        def round_pairs(pairs, z_turned):
             nc.scalar.copy(
                 pairs.rearrange("s (b p e) -> s b p e", p=P, e=2),
                 z_turned[:].rearrange("s b e p -> s b p e"),
             )
 
-        def turn_back(back, u, pairs, first, blocks):
-            for b in range(blocks):
-                words = pairs[:, (first + b) * 2 * P : (first + b + 1) * 2 * P].bitcast(F32)
-                nc.tensor.transpose(back[:, b, u, :], words, identity[:])
+        def turn_back(back, u, pairs, block):
+            words = pairs[:, block * 2 * P : (block + 1) * 2 * P].bitcast(F32)
+            nc.tensor.transpose(back[:, u, :], words, identity[:])
 
-        out_view = out.rearrange("(g p) s -> p g s", p=P)
+        out_rows = out.rearrange("(g p) s -> p g s", p=P)
 
         def second_product(z_bf, tokens, ways_out, name):
             width = tokens.stop - tokens.start
-            z_codes = keep.tile([P, width], U32, name="z_codes" + name, align_bytes=64)
-            z_scales = keep.tile([P, width], U8, name="z_scales" + name, align_bytes=64)
+            z_codes = keep.tile([P, width], U32, name="z_codes_" + name, align_bytes=64)
+            z_scales = keep.tile([P, width], U8, name="z_scales_" + name, align_bytes=64)
             nc.vector.quantize_mx(out=z_codes[:].bitcast(FP8X4), scales=z_scales[:], in_=z_bf[:])
-            per_bank = PACK // len(ways_out)
-            for i, (number, copy, queue) in enumerate(ways_out):
-                acc = bank(number, [P, per_bank, width], "acc")
-                for g in range(per_bank):
-                    rows = slice((i * per_bank + g) * P, (i * per_bank + g + 1) * P)
+            groups = N // P // len(ways_out)
+            for way, (number, copy, queue) in enumerate(ways_out):
+                acc = bank(number, [P, groups, width], "acc")
+                for g in range(groups):
+                    rows = slice((way * groups + g) * P, (way * groups + g + 1) * P)
                     nc.tensor.matmul_mx(
                         out=acc[:, g, :],
                         lhsT=w2_codes[:, rows].bitcast(FP8X4),
@@ -214,77 +195,82 @@ def tile_picked_kan8_none_p_kernel(
                         start=True,
                         stop=True,
                     )
-                result = keep.tile([P, per_bank, width], F32, name="result%s_%d" % (name, i))
+                result = keep.tile([P, groups, width], F32, name="result_%s%d" % (name, way))
                 copy(result[:], acc[:])
-                queue.dma_start(out_view[:, i * per_bank : (i + 1) * per_bank, tokens], result[:])
+                queue.dma_start(out_rows[:, way * groups : (way + 1) * groups, tokens], result[:])
 
-        on_scalar, on_vector = nc.scalar.copy, nc.vector.tensor_copy
+        z_low = [bank(4 + h, [P, HALF // P, 2, P], "z_low") for h in range(2)]
+        for t in low_slots:
+            for knot in outer_knots:
+                for tokens in halves if (t, knot) == (low_slots[0], outer_knots[0]) else [all_tokens]:
+                    make_term(terms_low[:, t, knot, tokens], t, knot, tokens)
+            for block in range(S // P):
+                h, b = divmod(block, HALF // P)
+                for i, knot in enumerate((middle_knot,) + outer_knots):
+                    term = terms_low[:, t, knot, block * P : (block + 1) * P]
+                    add_turned(z_low[h][:, b, t, :], term, i == 0, i == KNOTS - 1)
 
-        z_low = [bank(4 + h, [P, 2, 2, P], "z_low") for h in range(2)]
-        product(1, 0, slice(0, S), terms_low[:, 1, 0, :])
-        product(1, 2, slice(0, S), terms_low[:, 1, 2, :])
-        for h in range(2):
-            add_turned(z_low[h], 1, [terms_low[:, 1, k, halves[h]] for k in range(3)])
-        for k in (0, 2):
-            product(0, k, slice(0, S), terms_low[:, 0, k, :])
-        for h in range(2):
-            add_turned(z_low[h], 0, [terms_low[:, 0, k, halves[h]] for k in (1, 0, 2)])
-        prepare_w2()
-        pairs_low = keep.tile([P, S * 2], BF16, name="pairs_low", tag="w2_then_pairs")
-        for h in range(2):
-            round_pairs(z_low[h], pairs_low[:, h * S : (h + 1) * S])
+        w2_to = w2_bf[:].rearrange("p (c i j) -> p c j i", i=4, j=PACK)
+        w2_from = w2_raw[:].rearrange("p j (c i) -> p c j i", i=4)
+        for part in range(2):
+            columns = slice(part * N // 8, (part + 1) * N // 8)
+            nc.scalar.copy(w2_to[:, columns], w2_from[:, columns])
+        nc.vector.quantize_mx(out=w2_codes[:].bitcast(FP8X4), scales=w2_scales[:], in_=w2_bf[:])
 
-        def upper_slots(tokens, z_banks, back_banks, name, terms_tag, z_tag):
+        pairs_low = keep.tile([P, 2 * S], BF16, name="pairs_low", tag="w2_raw_then_pairs")
+        for h in range(2):
+            round_pairs(pairs_low[:, h * 2 * HALF : (h + 1) * 2 * HALF], z_low[h])
+
+        def finish_z(tokens, z_banks, back_banks, name, terms_tag, z_tag):
             width = tokens.stop - tokens.start
             blocks = width // P
-            back = [bank(number, [P, 1, 2, P], "back") for number in back_banks]
+            back = [bank(number, [P, 2, P], "back") for number in back_banks]
             for b in range(blocks):
-                turn_back(back[b], 0, pairs_low, tokens.start // P + b, 1)
+                turn_back(back[b], 0, pairs_low, tokens.start // P + b)
             z_high = [bank(number, [P, 1, 2, P], "z_high") for number in z_banks]
-            terms = keep.tile([P, 2, 3, width], F32, name="terms" + name, tag=terms_tag, align_bytes=64)
-            for e in range(2):
-                for k in range(3):
-                    product(2 + e, k, tokens, terms[:, e, k, :])
+            terms = keep.tile([P, 2, KNOTS, width], F32, name="terms_" + name, tag=terms_tag, align_bytes=64)
+            for e, t in enumerate(high_slots):
+                for knot in range(KNOTS):
+                    make_term(terms[:, e, knot, :], t, knot, tokens)
                     for b in range(blocks):
-                        nc.tensor.matmul(
-                            z_high[b][:, 0, e, :],
-                            terms[:, e, k, b * P : (b + 1) * P],
-                            identity[:],
-                            start=(k == 0),
-                            stop=(k == 2),
-                            is_transpose=True,
-                        )
-            pairs_high = keep.tile([P, width * 2], BF16, name="pairs_high" + name)
-            z_bf = keep.tile([P, PACK * width], BF16, name="z_bf" + name, tag=z_tag, align_bytes=64)
+                        term = terms[:, e, knot, b * P : (b + 1) * P]
+                        add_turned(z_high[b][:, 0, e, :], term, knot == 0, knot == KNOTS - 1)
+            pairs_high = keep.tile([P, 2 * width], BF16, name="pairs_high_" + name)
+            z_bf = keep.tile([P, PACK * width], BF16, name="z_bf_" + name, tag=z_tag, align_bytes=64)
             for b in range(blocks):
-                round_pairs(z_high[b], pairs_high[:, b * 2 * P : (b + 1) * 2 * P])
-                turn_back(back[b], 1, pairs_high, b, 1)
+                round_pairs(pairs_high[:, b * 2 * P : (b + 1) * 2 * P], z_high[b])
+                turn_back(back[b], 1, pairs_high, b)
             for b in range(blocks):
                 nc.scalar.copy(
                     z_bf[:, b * PACK * P : (b + 1) * PACK * P].bitcast(F32).rearrange("p (s u) -> p s u", u=2),
-                    back[b][:, 0].rearrange("p u s -> p s u"),
+                    back[b][:].rearrange("p u s -> p s u"),
                 )
             return z_bf
 
-        first, second, last = slice(0, 256), slice(256, 384), slice(384, 512)
-        z_first = upper_slots(first, (2, 3), (0, 4), "a", "terms_a", "before_c")
-        z_second = upper_slots(second, (7,), (1,), "b", "before_b", "z_b")
-        second_product(z_first, first, ((5, on_scalar, nc.sync), (4, on_scalar, nc.sync)), "a")
-        back = bank(6, [P, 1, 2, P], "back")
-        turn_back(back, 0, pairs_low, 3, 1)
+        first, second, last = slice(0, HALF), slice(HALF, HALF + P), slice(HALF + P, S)
+        by_scalar, by_vector = nc.scalar.copy, nc.vector.tensor_copy
+        z_first = finish_z(first, (2, 3), (0, 4), "first", "terms_first", "z_first_then_terms")
+        z_second = finish_z(second, (7,), (1,), "second", "w2_bf_then_terms", "z_second")
+        second_product(z_first, first, ((5, by_scalar, nc.sync), (4, by_scalar, nc.sync)), "first")
+
+        back_last = bank(6, [P, 2, P], "back")
+        turn_back(back_last, 0, pairs_low, last.start // P)
         z_last = keep.tile([P, PACK * P], BF16, name="z_last", align_bytes=64)
-        nc.scalar.copy(z_last[:].bitcast(F32).rearrange("p (s u) -> p s u", u=2)[:, :, 0], back[:, 0, 0, :])
-        terms_last = keep.tile([P, 3, 2, P], F32, name="terms_c", tag="before_c", align_bytes=64)
+        nc.scalar.copy(z_last[:].bitcast(F32).rearrange("p (s u) -> p s u", u=2)[:, :, 0], back_last[:, 0, :])
+        terms_last = keep.tile([P, KNOTS, 2, P], F32, name="terms_last", tag="z_first_then_terms", align_bytes=64)
         partial = keep.tile([P, 2, P], F32, name="partial")
-        for k, e in ((0, 0), (0, 1), (1, 0), (1, 1), (2, 0)):
-            product(2 + e, k, last, terms_last[:, k, e, :])
+        for knot in range(KNOTS - 1):
+            for e, t in enumerate(high_slots):
+                make_term(terms_last[:, knot, e, :], t, knot, last)
+        make_term(terms_last[:, 2, 0, :], high_slots[0], 2, last)
         nc.vector.tensor_tensor(partial[:], terms_last[:, 0], terms_last[:, 1], ADD)
-        product(3, 2, last, terms_last[:, 2, 1, :])
-        second_product(z_second, second, ((6, on_scalar, nc.sync),), "b")
+        make_term(terms_last[:, 2, 1, :], high_slots[1], 2, last)
+        second_product(z_second, second, ((6, by_scalar, nc.sync),), "second")
         nc.vector.tensor_tensor(
             z_last[:].rearrange("p (s u e) -> p s u e", u=2, e=2)[:, :, 1, :],
             partial[:].rearrange("p e s -> p s e"),
             terms_last[:, 2].rearrange("p e s -> p s e"),
             ADD,
         )
-        second_product(z_last, last, ((3, on_vector, nc.sync), (7, on_scalar, nc.scalar)), "c")
+        last_ways = ((3, by_vector, nc.sync), (7, by_scalar, nc.scalar), (0, by_vector, nc.sync), (2, by_scalar, nc.scalar))
+        second_product(z_last, last, last_ways, "last")

from contextlib import ExitStack

import concourse.mybir as mybir
from concourse.masks import make_identity

F32 = mybir.dt.float32
BF16 = mybir.dt.bfloat16
I32 = mybir.dt.int32
U32 = mybir.dt.uint32
U16 = mybir.dt.uint16
U8 = mybir.dt.uint8
FP8X4 = mybir.dt.float8_e4m3fn_x4
RELU = mybir.ActivationFunctionType.Relu
MULT = mybir.AluOpType.mult
ADD = mybir.AluOpType.add
MAX = mybir.AluOpType.max

K, T, S, H, N, U = 512, 2048, 512, 512, 512, 512
FLOPS = 2 * K * H * S + 2 * H * N * S

P = 128
PACK = 4
GROUP = 16
QUADRANT = 32
KNOTS = 3
KNOT_DISTANCE = 0.75
HALF = S // 2
W1_GROUPS_ON_VECTOR = 72


def tile_picked_kan8_none_p_kernel(
    tc, x_words, x_scales, w1, cf1, cf2, cf3, w2, offs, fn, out
):
    nc = tc.nc
    with ExitStack() as ctx:
        lists = ctx.enter_context(tc.tile_pool(name="lists", bufs=1))
        keep = ctx.enter_context(tc.tile_pool(name="keep", bufs=1))
        psum = ctx.enter_context(tc.psum_pool(name="psum", bufs=1))

        def bank(number, shape, name):
            return psum.tile(shape, F32, name=name, tag="bank%d" % number)

        def entries(list_tile, tokens):
            return list_tile[:, tokens.start // GROUP : tokens.stop // GROUP]

        all_tokens = slice(0, S)
        halves = [slice(0, HALF), slice(HALF, S)]
        low_slots, high_slots = (0, 1), (2, 3)
        middle_knot, outer_knots = 1, (0, 2)

        offs_sb = lists.tile([P, S // GROUP], U16, name="offs_sb")
        fn_sb = lists.tile([P, S // GROUP], U16, name="fn_sb")
        scale_window = keep.tile([P, T], U8, name="scale_window")
        word_window = keep.tile([P, T], I32, name="word_window")
        w1_raw = keep.tile([P, PACK, H], F32, name="w1_raw")
        w2_raw = keep.tile([P, PACK, N], F32, name="w2_raw", tag="w2_raw_then_pairs")
        tables = [
            [
                keep.tile([P, 2 * U if t in low_slots else U], F32, name="cf%d_%d" % (knot, t))
                for knot in range(KNOTS)
            ]
            for t in range(PACK)
        ]

        def load_table(t, knot):
            rows = (cf1, cf2, cf3)[knot].rearrange("(p t) c -> t p c", t=PACK)[t]
            nc.sync.dma_start(tables[t][knot][:, :U], rows)

        nc.vector.memset(scale_window[:].bitcast(I32), 0)
        nc.sync.dma_start(fn_sb[:], fn)
        load_table(0, middle_knot)
        nc.sync.dma_start(offs_sb[:], offs)
        scale_rows = x_scales[0].bitcast(I32).rearrange("(q r) c -> r q c", q=P // QUADRANT)
        for r in range(QUADRANT // 8):
            nc.sync.dma_start(scale_window[r:P:QUADRANT, :].bitcast(I32), scale_rows[r])
        load_table(1, middle_knot)
        nc.sync.dma_start(w1_raw[:], w1.rearrange("(p j) c -> p j c", j=PACK))
        nc.sync.dma_start(word_window[:], x_words[0].rearrange("p n t -> p (n t)").bitcast(I32))
        for t in low_slots:
            for knot in outer_knots:
                load_table(t, knot)
        nc.sync.dma_start(w2_raw[:], w2.rearrange("(p j) c -> p j c", j=PACK))
        for t in high_slots:
            for knot in range(KNOTS):
                load_table(t, knot)

        shift_down = keep.tile([P, 1], F32, name="shift_down")
        shift_none = keep.tile([P, 1], F32, name="shift_none")
        shift_up = keep.tile([P, 1], F32, name="shift_up")
        nc.vector.memset(shift_down[:], -KNOT_DISTANCE)
        nc.vector.memset(shift_none[:], 0.0)
        nc.scalar.activation(shift_up[:], shift_down[:], RELU, bias=shift_none[:], scale=-1.0)
        shifts = (shift_up, shift_none, shift_down)
        identity = keep.tile([P, P], F32, name="identity")
        make_identity(nc, identity[:])

        early_slopes = keep.tile([P, len(low_slots), S], F32, name="early_slopes")
        for t in low_slots:
            nc.vector.tensor_copy(early_slopes[:, t, :], tables[t][middle_knot][:].indirect(fn_sb[:]))

        w1_bf = keep.tile([P, PACK * H], BF16, name="w1_bf", align_bytes=64)
        w1_codes = keep.tile([P, H], U32, name="w1_codes", align_bytes=64)
        w1_scales = keep.tile([P, H], U8, name="w1_scales", align_bytes=64)
        w1_to = w1_bf[:].rearrange("p (t m j) -> p m t j", t=PACK, j=PACK)
        w1_from = w1_raw[:].rearrange("p j (m t) -> p m t j", t=PACK)
        nc.vector.tensor_copy(w1_to[:, :W1_GROUPS_ON_VECTOR], w1_from[:, :W1_GROUPS_ON_VECTOR])
        nc.scalar.copy(w1_to[:, W1_GROUPS_ON_VECTOR:], w1_from[:, W1_GROUPS_ON_VECTOR:])

        x_scale = keep.tile([P, S], U8, name="x_scale", align_bytes=64)
        nc.vector.tensor_copy(x_scale[:], scale_window[:].indirect(offs_sb[:]))
        nc.vector.quantize_mx(out=w1_codes[:].bitcast(FP8X4), scales=w1_scales[:], in_=w1_bf[:])
        x_codes = [keep.tile([P, HALF], U32, name="x_codes%d" % h, align_bytes=64) for h in range(2)]

        def first_product(y, t, h):
            features = slice(t * P, (t + 1) * P)
            nc.tensor.matmul_mx(
                out=y,
                lhsT=w1_codes[:, features].bitcast(FP8X4),
                lhsT_scale=w1_scales[:, features],
                rhs=x_codes[h][:].bitcast(FP8X4),
                rhs_scale=x_scale[:, halves[h]],
                start=True,
                stop=True,
            )

        y_low = [[bank(2 * h + t, [P, HALF], "y_low") for t in low_slots] for h in range(2)]
        y_high = [bank(6 + e, [P, S], "y_high") for e in range(2)]
        for h in range(2):
            nc.vector.tensor_copy(x_codes[h][:], word_window[:].bitcast(U32).indirect(entries(offs_sb, halves[h])))
            for t in low_slots:
                first_product(y_low[h][t][:], t, h)
        for e, t in enumerate(high_slots):
            for h in range(2):
                first_product(y_high[e][:, halves[h]], t, h)

        ramps = [keep.tile([P, PACK, S], F32, name="ramps%d" % knot) for knot in range(KNOTS)]
        terms_low = keep.tile([P, len(low_slots), KNOTS, S], F32, name="terms_low")
        for h in range(2):
            for t in low_slots:
                nc.vector.scalar_tensor_tensor(
                    terms_low[:, t, middle_knot, halves[h]],
                    y_low[h][t][:],
                    0.0,
                    early_slopes[:, t, halves[h]],
                    MAX,
                    MULT,
                )
        for t in low_slots:
            for h in range(2):
                for knot in outer_knots:
                    nc.scalar.activation(ramps[knot][:, t, halves[h]], y_low[h][t][:], RELU, bias=shifts[knot][:])
        for e, t in enumerate(high_slots):
            for knot in range(KNOTS):
                nc.scalar.activation(ramps[knot][:, t, :], y_high[e][:], RELU, bias=shifts[knot][:])

        w2_bf = keep.tile([P, PACK * N], BF16, name="w2_bf", tag="w2_bf_then_terms", align_bytes=64)
        w2_codes = keep.tile([P, N], U32, name="w2_codes", align_bytes=64)
        w2_scales = keep.tile([P, N], U8, name="w2_scales", align_bytes=64)

        def make_term(term, t, knot, tokens):
            window = tables[t][knot][:].indirect(entries(fn_sb, tokens))
            nc.vector.tensor_tensor(term, window, ramps[knot][:, t, tokens], MULT)

        def add_turned(z_turned, term, first, last):
            nc.tensor.matmul(z_turned, term, identity[:], start=first, stop=last, is_transpose=True)

        def round_pairs(pairs, z_turned):
            nc.scalar.copy(
                pairs.rearrange("s (b p e) -> s b p e", p=P, e=2),
                z_turned[:].rearrange("s b e p -> s b p e"),
            )

        def turn_back(back, u, pairs, block):
            words = pairs[:, block * 2 * P : (block + 1) * 2 * P].bitcast(F32)
            nc.tensor.transpose(back[:, u, :], words, identity[:])

        out_rows = out.rearrange("(g p) s -> p g s", p=P)

        def second_product(z_bf, tokens, ways_out, name):
            width = tokens.stop - tokens.start
            z_codes = keep.tile([P, width], U32, name="z_codes_" + name, align_bytes=64)
            z_scales = keep.tile([P, width], U8, name="z_scales_" + name, align_bytes=64)
            nc.vector.quantize_mx(out=z_codes[:].bitcast(FP8X4), scales=z_scales[:], in_=z_bf[:])
            groups = N // P // len(ways_out)
            for way, (number, copy, queue) in enumerate(ways_out):
                acc = bank(number, [P, groups, width], "acc")
                for g in range(groups):
                    rows = slice((way * groups + g) * P, (way * groups + g + 1) * P)
                    nc.tensor.matmul_mx(
                        out=acc[:, g, :],
                        lhsT=w2_codes[:, rows].bitcast(FP8X4),
                        lhsT_scale=w2_scales[:, rows],
                        rhs=z_codes[:].bitcast(FP8X4),
                        rhs_scale=z_scales[:],
                        start=True,
                        stop=True,
                    )
                result = keep.tile([P, groups, width], F32, name="result_%s%d" % (name, way))
                copy(result[:], acc[:])
                queue.dma_start(out_rows[:, way * groups : (way + 1) * groups, tokens], result[:])

        z_low = [bank(4 + h, [P, HALF // P, 2, P], "z_low") for h in range(2)]
        for t in low_slots:
            for knot in outer_knots:
                for tokens in halves if (t, knot) == (low_slots[0], outer_knots[0]) else [all_tokens]:
                    make_term(terms_low[:, t, knot, tokens], t, knot, tokens)
            for block in range(S // P):
                h, b = divmod(block, HALF // P)
                for i, knot in enumerate((middle_knot,) + outer_knots):
                    term = terms_low[:, t, knot, block * P : (block + 1) * P]
                    add_turned(z_low[h][:, b, t, :], term, i == 0, i == KNOTS - 1)

        w2_to = w2_bf[:].rearrange("p (c i j) -> p c j i", i=4, j=PACK)
        w2_from = w2_raw[:].rearrange("p j (c i) -> p c j i", i=4)
        for part in range(2):
            columns = slice(part * N // 8, (part + 1) * N // 8)
            nc.scalar.copy(w2_to[:, columns], w2_from[:, columns])
        nc.vector.quantize_mx(out=w2_codes[:].bitcast(FP8X4), scales=w2_scales[:], in_=w2_bf[:])

        pairs_low = keep.tile([P, 2 * S], BF16, name="pairs_low", tag="w2_raw_then_pairs")
        for h in range(2):
            round_pairs(pairs_low[:, h * 2 * HALF : (h + 1) * 2 * HALF], z_low[h])

        def finish_z(tokens, z_banks, back_banks, name, terms_tag, z_tag):
            width = tokens.stop - tokens.start
            blocks = width // P
            back = [bank(number, [P, 2, P], "back") for number in back_banks]
            for b in range(blocks):
                turn_back(back[b], 0, pairs_low, tokens.start // P + b)
            z_high = [bank(number, [P, 1, 2, P], "z_high") for number in z_banks]
            terms = keep.tile([P, 2, KNOTS, width], F32, name="terms_" + name, tag=terms_tag, align_bytes=64)
            for e, t in enumerate(high_slots):
                for knot in range(KNOTS):
                    make_term(terms[:, e, knot, :], t, knot, tokens)
                    for b in range(blocks):
                        term = terms[:, e, knot, b * P : (b + 1) * P]
                        add_turned(z_high[b][:, 0, e, :], term, knot == 0, knot == KNOTS - 1)
            pairs_high = keep.tile([P, 2 * width], BF16, name="pairs_high_" + name)
            z_bf = keep.tile([P, PACK * width], BF16, name="z_bf_" + name, tag=z_tag, align_bytes=64)
            for b in range(blocks):
                round_pairs(pairs_high[:, b * 2 * P : (b + 1) * 2 * P], z_high[b])
                turn_back(back[b], 1, pairs_high, b)
            for b in range(blocks):
                nc.scalar.copy(
                    z_bf[:, b * PACK * P : (b + 1) * PACK * P].bitcast(F32).rearrange("p (s u) -> p s u", u=2),
                    back[b][:].rearrange("p u s -> p s u"),
                )
            return z_bf

        first, second, last = slice(0, HALF), slice(HALF, HALF + P), slice(HALF + P, S)
        by_scalar, by_vector = nc.scalar.copy, nc.vector.tensor_copy
        z_first = finish_z(first, (2, 3), (0, 4), "first", "terms_first", "z_first_then_terms")
        z_second = finish_z(second, (7,), (1,), "second", "w2_bf_then_terms", "z_second")
        second_product(z_first, first, ((5, by_scalar, nc.sync), (4, by_scalar, nc.sync)), "first")

        back_last = bank(6, [P, 2, P], "back")
        turn_back(back_last, 0, pairs_low, last.start // P)
        z_last = keep.tile([P, PACK * P], BF16, name="z_last", align_bytes=64)
        nc.scalar.copy(z_last[:].bitcast(F32).rearrange("p (s u) -> p s u", u=2)[:, :, 0], back_last[:, 0, :])
        terms_last = keep.tile([P, KNOTS, 2, P], F32, name="terms_last", tag="z_first_then_terms", align_bytes=64)
        partial = keep.tile([P, 2, P], F32, name="partial")
        for knot in range(KNOTS - 1):
            for e, t in enumerate(high_slots):
                make_term(terms_last[:, knot, e, :], t, knot, last)
        make_term(terms_last[:, 2, 0, :], high_slots[0], 2, last)
        nc.vector.tensor_tensor(partial[:], terms_last[:, 0], terms_last[:, 1], ADD)
        make_term(terms_last[:, 2, 1, :], high_slots[1], 2, last)
        second_product(z_second, second, ((6, by_scalar, nc.sync),), "second")
        nc.vector.tensor_tensor(
            z_last[:].rearrange("p (s u e) -> p s u e", u=2, e=2)[:, :, 1, :],
            partial[:].rearrange("p e s -> p s e"),
            terms_last[:, 2].rearrange("p e s -> p s e"),
            ADD,
        )
        last_ways = ((3, by_vector, nc.sync), (7, by_scalar, nc.scalar), (0, by_vector, nc.sync), (2, by_scalar, nc.scalar))
        second_product(z_last, last, last_ways, "last")
